import numpy as np
import ml_dtypes


def mxq(x, axis, fmt="e4m3"):
    dtype, down = {"e4m3": (ml_dtypes.float8_e4m3fn, 7), "e5m2": (ml_dtypes.float8_e5m2, 14)}[fmt]
    v = np.moveaxis(np.asarray(x, np.float32).astype(ml_dtypes.bfloat16).astype(np.float64), axis, -1)
    blocks = v.reshape(v.shape[:-1] + (-1, 32))
    amax = np.abs(blocks).max(-1, keepdims=True)
    byte = np.maximum(np.where(amax > 0, np.frexp(amax)[1] - 1 + 127, 0) - down, 1)
    scale = np.exp2(byte - 127.0)
    codes = (blocks / scale).astype(np.float32).astype(dtype).astype(np.float64)
    return np.moveaxis((codes * scale).reshape(v.shape), -1, axis)


WIDE = False


def mx_kscale(k):
    if not WIDE:
        return np.ones(k)
    levels = np.array([10, -10, 5, -5, 0])
    if k % 512:
        return np.exp2(np.random.permutation(np.resize(levels, k // 32))).repeat(32)
    a = np.empty((k // 512, 16))
    for p in range(k // 512):
        a[p, :8] = np.random.permutation(np.resize(levels, 8))
        for g in range(8):
            far = levels[np.abs(levels - a[p, g]) >= 10]
            a[p, g + 8] = far[np.random.randint(len(far))]
    return np.exp2(a.ravel()).repeat(32)


def f64(x):
    return np.asarray(x).astype(np.float64)


def striped(idx):
    return np.tile(idx.reshape(-1, 16).T, (8, 1)).astype(np.uint16)


def unstriped(offs):
    return offs[:16].T.reshape(-1).astype(np.int64)


def striped8(idx):
    return np.concatenate([x.reshape(-1, 16).T for x in idx]).astype(np.uint16)


def runs(offs, k):
    lists = np.stack([offs[16 * r : 16 * r + 16].T.reshape(-1) for r in range(8)]).astype(np.int64)
    return lists[np.arange(k) % 512 // 64]


def pack_weight(w):
    k, n = w.shape
    w = f64(np.asarray(w, np.float32).astype(ml_dtypes.bfloat16)).reshape(k // 32, 32, n)
    amax = np.abs(w).max(1)
    byte = np.clip(np.where(amax > 0, np.frexp(amax)[1] - 1 + 127 - 7, 1), 1, 254)
    scaled = (w * np.exp2(127.0 - byte)[:, None, :]).reshape(k, n).astype(np.float32)
    words = np.ascontiguousarray(scaled.reshape(k // 512, 128, 4, n).transpose(0, 1, 3, 2)).astype(ml_dtypes.float8_e4m3fn).view(np.uint8)
    return words, np.ascontiguousarray(byte.astype(np.uint8).reshape(k // 512, 16, n))


def unpack_weight(words, scales):
    g, p, n, _ = words.shape
    vals = np.ascontiguousarray(words).view(ml_dtypes.float8_e4m3fn).astype(np.float64) * np.repeat(np.exp2(scales.astype(np.float64) - 127.0), 8, axis=1)[..., None]
    return vals.transpose(0, 1, 3, 2).reshape(g * 512, n)


def sigmoid(v):
    return 1.0 / (1.0 + np.exp(-np.maximum(v, -700.0)))


K, T, S, N, H, G, W = 512, 1024, 512, 512, 512, 2048, 1024


def setup_inputs():
    n = np.random.standard_normal
    s = mx_kscale(K)[:, None]
    u = mx_kscale(S)
    packed_xT = pack_weight(n((K, T)) * s)
    packed_dT = pack_weight(n((K, G)) / s)
    return {
        "x_words": packed_xT[0],
        "x_scales": packed_xT[1],
        "w1": (n((K, H)) / np.sqrt(K) / s).astype(np.float32),
        "d_words": packed_dT[0],
        "d_scales": packed_dT[1],
        "gn": (np.random.uniform(0.5, 1.5, (H, 1)) * u[:, None]).astype(np.float32),
        "gk": (np.random.uniform(0.5, 1.5, (H, 1)) * u[:, None]).astype(np.float32),
        "w2": (n((H, N)) / np.sqrt(2 * H) / u[:, None]).astype(np.float32),
        "w3": (n((H, N)) / np.sqrt(2 * H) / u[:, None]).astype(np.float32),
        "offs": striped(np.random.permutation(T)[:S]),
        "kidx": striped8(np.random.randint(0, G, (8, H))),
        "two": striped(np.random.permutation(T)[:S]),
        "n1": striped8(np.stack([np.random.permutation(S) for _ in range(8)])),
        "n2": striped8(np.stack([np.random.permutation(S) for _ in range(8)])),
        "n3": striped8(np.stack([np.random.permutation(S) for _ in range(8)])),
        "n4": striped(np.random.permutation(S)),
        "n5": striped(np.random.permutation(S)),
        "n6": striped(np.random.randint(0, S, W)),
    }


def reference(x_words, x_scales, w1, d_words, d_scales, gn, gk, w2, w3, offs, kidx, two, n1, n2, n3, n4, n5, n6):
    xq = unpack_weight(x_words, x_scales)[:, unstriped(offs)]
    y = mxq(f64(w1), 0, "e4m3").T @ xq
    z = f64(gn) * (np.maximum(y, y[np.arange(H)[:, None], runs(n1, H)]) - (np.maximum(y[np.arange(H)[:, None], runs(n2, H)], y[np.arange(H)[:, None], runs(n3, H)])))
    d_kidx = unpack_weight(d_words, d_scales)[np.arange(K)[:, None], runs(kidx, K)]
    x_two = unpack_weight(x_words, x_scales)[:, unstriped(two)]
    s = 0.0625 * (d_kidx.T @ x_two)
    st = s * (sigmoid(s[:, unstriped(n4)]))
    z2 = f64(gk) * (st - st[:, unstriped(n5)])
    h = mxq(f64(w2), 0, "e4m3").T @ mxq(z, 0, "e4m3") + mxq(f64(w3), 0, "e4m3").T @ mxq(z2, 0, "e4m3")
    mb = h[:, unstriped(n6)]
    ms = mb.reshape(N, S, 2).sum(axis=2)
    mx = mb.reshape(N, S, 2).max(axis=2)
    return ms - np.maximum(h, mx)

@@ -1,0 +1,269 @@
+from contextlib import ExitStack
+
+import concourse.mybir as mybir
+
+K, T, S, N, H, G, W = 512, 1024, 512, 512, 512, 2048, 1024
+FLOPS = 4 * 2 * 512 * 512 * 512
+
+F32 = mybir.dt.float32
+BF16 = mybir.dt.bfloat16
+I32 = mybir.dt.int32
+U32 = mybir.dt.uint32
+U16 = mybir.dt.uint16
+U8 = mybir.dt.uint8
+FP8X4 = mybir.dt.float8_e4m3fn_x4
+ALU = mybir.AluOpType
+ACT = mybir.ActivationFunctionType
+
+P = 128
+PACK = 4
+WIDE = 2 * S
+NARROW = S + 16
+FUSED_TILES = (0, 1, 2)
+
+
+def tile_picked_jkeymixhopggpair_none_p_kernel(
+    tc, x_words, x_scales, w1, d_words, d_scales, gn, gk, w2, w3, offs, kidx, two, n1, n2, n3, n4, n5, n6, out
+):
+    nc = tc.nc
+    with ExitStack() as ctx:
+        lists = ctx.enter_context(tc.tile_pool(name="lists", bufs=1))
+        keep = ctx.enter_context(tc.tile_pool(name="keep", bufs=1))
+        ring = ctx.enter_context(tc.tile_pool(name="ring", bufs=4))
+        psum = ctx.enter_context(tc.psum_pool(name="psum", bufs=1))
+
+        def load_list(name, src):
+            t = lists.tile(list(src.shape), U16, name=name)
+            nc.sync.dma_start(t[:], src)
+            return t
+
+        def mx_tiles(name, width):
+            words = keep.tile([P, width], U32, name=name + "_words", align_bytes=64)
+            scales = keep.tile([P, width], U8, name=name + "_scales", align_bytes=64)
+            return words, scales
+
+        def quantize(dst, src, cols):
+            words, scales = dst
+            nc.vector.quantize_mx(
+                out=words[:, cols].bitcast(FP8X4),
+                scales=scales[:, cols],
+                in_=src[:, PACK * cols.start : PACK * cols.stop],
+            )
+
+        def product(acc, lhs, tile_index, rhs, start, stop):
+            cols = slice(P * tile_index, P * (tile_index + 1))
+            nc.tensor.matmul_mx(
+                out=acc[:],
+                lhsT=lhs[0][:, cols].bitcast(FP8X4),
+                lhsT_scale=lhs[1][:, cols],
+                rhs=rhs[0][:].bitcast(FP8X4),
+                rhs_scale=rhs[1][:],
+                start=start,
+                stop=stop,
+            )
+
+        x_tab = mx_tiles("x_tab", T)
+        d_tab = mx_tiles("d_tab", G)
+        nc.vector.memset(d_tab[1][:].bitcast(I32), 0)
+        offs_t = load_list("offs_t", offs)
+        x_rows = x_scales[0].bitcast(I32).rearrange("(q r) c -> r q c", r=4)
+        for r in range(4):
+            nc.scalar.dma_start(x_tab[1][r:P:4, :].bitcast(I32), x_rows[r].unsqueeze(1).to_broadcast([4, 8, T // 4]))
+        nc.sync.dma_start(x_tab[0][:].bitcast(I32), x_words[0].rearrange("p n t -> p (n t)").bitcast(I32))
+        half = H // 2
+        w1_raw = [keep.tile([P, PACK, half], F32, name="w1_raw%d" % a) for a in range(2)]
+        for a in range(2):
+            nc.sync.dma_start(w1_raw[a][:], w1[:, half * a : half * (a + 1)].rearrange("(p j) c -> p j c", j=PACK))
+        two_t = load_list("two_t", two)
+        kidx_t = load_list("kidx_t", kidx)
+        d_rows = d_scales[0].bitcast(I32).rearrange("(g e) c -> e g c", e=2)
+        for e in range(2):
+            nc.scalar.dma_start(d_tab[1][e:P:16, :].bitcast(I32), d_rows[e])
+        nc.sync.dma_start(d_tab[0][:].bitcast(I32), d_words[0].rearrange("p n t -> p (n t)").bitcast(I32))
+        n1_t = load_list("n1_t", n1)
+        n2_t = load_list("n2_t", n2)
+        n3_t = load_list("n3_t", n3)
+        n4_t = load_list("n4_t", n4)
+        n5_t = load_list("n5_t", n5)
+        gn_t = keep.tile([P, PACK], F32, name="gn_t")
+        gk_t = keep.tile([P, PACK], F32, name="gk_t")
+        nc.sync.dma_start(gn_t[:], gn.rearrange("(p t) o -> p (t o)", t=PACK))
+        nc.sync.dma_start(gk_t[:], gk.rearrange("(p t) o -> p (t o)", t=PACK))
+        w3_raw = keep.tile([P, PACK, N], F32, name="w3_raw")
+        w2_raw = keep.tile([P, PACK, N], F32, name="w2_raw")
+        nc.sync.dma_start(w3_raw[:], w3.rearrange("(p j) c -> p j c", j=PACK))
+        nc.sync.dma_start(w2_raw[:], w2.rearrange("(p j) c -> p j c", j=PACK))
+        n6_t = load_list("n6_t", n6)
+
+        x_idx = mx_tiles("x_idx", S)
+        nc.vector.tensor_copy(x_idx[1][:], x_tab[1][:].indirect(offs_t[:]))
+        nc.vector.tensor_copy(x_idx[0][:], x_tab[0][:].indirect(offs_t[:]))
+
+        w1_bf = keep.tile([P, PACK * H], BF16, name="w1_bf", align_bytes=64)
+        w1_view = w1_bf[:].rearrange("p (t m j) -> p m j t", t=PACK, j=PACK)
+        for a in range(2):
+            nc.scalar.copy(
+                w1_view[:, (P // 2) * a : (P // 2) * (a + 1)],
+                w1_raw[a][:].rearrange("p j (m t) -> p m j t", t=PACK),
+            )
+
+        x_two = mx_tiles("x_two", S)
+        nc.vector.tensor_copy(x_two[0][:], x_tab[0][:].indirect(two_t[:]))
+        nc.vector.tensor_copy(x_two[1][:], x_tab[1][:].indirect(two_t[:]))
+        w1_q = mx_tiles("w1_q", H)
+        quantize(w1_q, w1_bf, slice(0, P))
+        quantize(w1_q, w1_bf, slice(P, 2 * P))
+        quantize(w1_q, w1_bf, slice(2 * P, 4 * P))
+        y_bank = [psum.tile([P, S], F32, name="y_bank%d" % t) for t in range(PACK)]
+        for t in range(PACK):
+            product(y_bank[t], w1_q, t, x_idx, True, True)
+
+        keys = mx_tiles("keys", H)
+        keys_dealt = mx_tiles("keys_dealt", H)
+        keys_plane = keep.tile([P, H], U8, name="keys_plane", align_bytes=64)
+        nc.vector.tensor_copy(keys[1][:], d_tab[1][:].indirect(kidx_t[:]))
+        nc.vector.tensor_copy(keys[0][:], d_tab[0][:].indirect(kidx_t[:]))
+        nc.vector.tensor_copy(
+            keys_dealt[1][:].rearrange("p (t m) -> p m t", t=PACK), keys[1][:].rearrange("p (m t) -> p m t", t=PACK)
+        )
+        nc.vector.tensor_copy(
+            keys_dealt[0][:].bitcast(I32).rearrange("p (t c i) -> p c t i", t=PACK, i=4),
+            keys[0][:].bitcast(I32).rearrange("p (c i t) -> p c t i", t=PACK, i=4),
+        )
+        nc.vector.tensor_copy(keys_plane[:].bitcast(I32), keys_dealt[1][:].bitcast(I32))
+        for e in range(2):
+            nc.sync.dma_start(keys_plane[2 + e : P : 32, :].bitcast(I32), keys_dealt[1][16 + e : P : 32, :].bitcast(I32))
+        s_bank = [psum.tile([P, S], F32, name="s_bank%d" % t) for t in range(PACK)]
+        for t in range(PACK):
+            product(s_bank[t], (keys_dealt[0], keys_plane), t, x_two, True, True)
+
+        minus_gn = keep.tile([P, PACK], F32, name="minus_gn")
+        nc.vector.tensor_scalar(minus_gn[:], gn_t[:], -1.0, None, ALU.mult)
+
+        halves = [slice(0, S // 2), slice(S // 2, S)]
+        minus_d = keep.tile([P, PACK, S], F32, name="minus_d")
+        st = keep.tile([P, PACK, WIDE], F32, name="st")
+        y, y_n1, left, y_n2, y_n3, s, gate = [], [], [], [], [], [], []
+        for t in range(PACK):
+            y.append(keep.tile([P, WIDE], F32, name="y%d" % t))
+            y_n1.append(keep.tile([P, S], F32, name="y_n1_%d" % t))
+            left.append(keep.tile([P, S], F32, name="left%d" % t))
+            y_n2.append(keep.tile([P, S], F32, name="y_n2_%d" % t))
+            y_n3.append(keep.tile([P, S], F32, name="y_n3_%d" % t))
+            s.append(keep.tile([P, WIDE], F32, name="s%d" % t, tag="s%d" % t, align_bytes=64))
+            gate.append(keep.tile([P, S], F32, name="gate%d" % t, tag="gate%d" % t))
+
+        for t in range(PACK):
+            nc.scalar.copy(y[t][:, :S], y_bank[t][:])
+            nc.scalar.activation(y_n1[t][:], y[t][:].indirect(n1_t[:]), ACT.Copy)
+            if t not in FUSED_TILES:
+                nc.scalar.activation(y_n2[t][:], y[t][:].indirect(n2_t[:]), ACT.Copy)
+                nc.scalar.activation(y_n3[t][:], y[t][:].indirect(n3_t[:]), ACT.Copy)
+        for t in range(PACK):
+            nc.scalar.activation(s[t][:, :S], s_bank[t][:], ACT.Copy, scale=0.0625)
+            nc.scalar.activation(gate[t][:], s[t][:].indirect(n4_t[:]), ACT.Sigmoid)
+
+        def left_step(t):
+            nc.vector.tensor_tensor(left[t][:], y[t][:, :S], y_n1[t][:], ALU.max)
+
+        def st_step(t):
+            nc.vector.scalar_tensor_tensor(st[:, t, :S], s[t][:, :S], gk_t[:, t : t + 1], gate[t][:], ALU.mult, ALU.mult)
+
+        left_step(0)
+        for t in FUSED_TILES:
+            nc.vector.tensor_tensor(y_n2[t][:], y[t][:].indirect(n2_t[:]), left[t][:], ALU.subtract)
+            nc.vector.tensor_tensor(y_n3[t][:], y[t][:].indirect(n3_t[:]), left[t][:], ALU.subtract)
+            left_step(t + 1)
+            nc.vector.tensor_tensor(minus_d[:, t, :], y_n2[t][:], y_n3[t][:], ALU.max)
+        done = 0
+        for t in range(len(FUSED_TILES), PACK):
+            right = ring.tile([P, S], F32, name="right")
+            nc.vector.tensor_tensor(right[:], y_n2[t][:], y_n3[t][:], ALU.max)
+            st_step(done)
+            done += 1
+            nc.vector.tensor_tensor(minus_d[:, t, :], right[:], left[t][:], ALU.subtract)
+            if t + 1 < PACK:
+                left_step(t + 1)
+        for t in range(done, PACK):
+            st_step(t)
+
+        st_n5 = [
+            keep.tile([P, PACK, S // 2], F32, name="st_n5_0"),
+            keep.tile([P, PACK, S // 2], F32, name="st_n5_1", tag="gate3"),
+        ]
+        for a in range(2):
+            for t in range(PACK):
+                nc.scalar.activation(st_n5[a][:, t, :], st[:, t, :].indirect(n5_t[:, 16 * a : 16 * (a + 1)]), ACT.Copy)
+
+        w_bf = keep.tile([P, PACK * 2 * PACK * P], BF16, name="w_bf", tag="s3", align_bytes=64)
+        w_q = mx_tiles("w_q", 2 * N)
+        for t in range(PACK):
+            for b, raw in enumerate((w2_raw, w3_raw)):
+                at = PACK * P * (2 * t + b)
+                nc.scalar.copy(
+                    w_bf[:, at : at + PACK * P].rearrange("p (c i j) -> p c j i", i=4, j=PACK),
+                    raw[:, :, P * t : P * (t + 1)].rearrange("p j (c i) -> p c j i", i=4),
+                )
+
+        z_bf = keep.tile([P, PACK * S], BF16, name="z_bf", align_bytes=64)
+        z2_bf = keep.tile([P, PACK * S], BF16, name="z2_bf", align_bytes=64)
+        z_q = mx_tiles("z_q", S)
+        z2_q = mx_tiles("z2_q", S)
+
+        def woven(bf, cols):
+            return bf[:, PACK * cols.start : PACK * cols.stop].rearrange("p (c i t) -> p c t i", i=4, t=PACK)
+
+        def planes(src):
+            return src.rearrange("p t (c i) -> p c t i", i=4)
+
+        gain = minus_gn[:].unsqueeze(1).unsqueeze(3).to_broadcast([P, S // 8, PACK, 4])
+        for cols in halves:
+            nc.vector.tensor_tensor(woven(z_bf, cols), planes(minus_d[:, :, cols]), gain, ALU.mult)
+        nc.vector.tensor_tensor(woven(z2_bf, halves[0]), planes(st[:, :, halves[0]]), planes(st_n5[0][:]), ALU.subtract)
+        quantize(z_q, z_bf, slice(0, S))
+        nc.vector.tensor_tensor(woven(z2_bf, halves[1]), planes(st[:, :, halves[1]]), planes(st_n5[1][:]), ALU.subtract)
+        quantize(z2_q, z2_bf, halves[0])
+        quantize(w_q, w_bf, slice(0, 2 * P))
+        quantize(z2_q, z2_bf, halves[1])
+        h_bank = [psum.tile([P, S], F32, name="y_bank%d" % t) for t in range(PACK)]
+        for t in range(PACK):
+            if t > 0:
+                quantize(w_q, w_bf, slice(2 * P * t, 2 * P * (t + 1)))
+            product(h_bank[t], w_q, 2 * t, z_q, True, False)
+            product(h_bank[t], w_q, 2 * t + 1, z2_q, False, True)
+
+        h = [keep.tile([P, NARROW], F32, name="h%d" % t) for t in range(PACK)]
+        members = [[keep.tile([P, S], F32, name="members%d_%d" % (t, a)) for a in range(2)] for t in range(PACK)]
+
+        def fetch(t):
+            for a in range(2):
+                window = h[t][:].indirect(n6_t[:, 32 * a : 32 * (a + 1)])
+                if t == 0:
+                    nc.vector.tensor_copy(members[t][a][:], window)
+                else:
+                    nc.scalar.activation(members[t][a][:], window, ACT.Copy)
+
+        def finish(t, which):
+            top = {a: ring.tile([P, S // 2], F32, name="top") for a in which}
+            rest = {a: ring.tile([P, S // 2], F32, name="rest") for a in which}
+            result = {a: ring.tile([P, S // 2], F32, name="result") for a in which}
+            for a in which:
+                nc.vector.tensor_tensor(top[a][:], h[t][:, halves[a]], members[t][a][:, 0::2], ALU.max)
+            for a in which:
+                nc.vector.tensor_tensor(rest[a][:], members[t][a][:, 1::2], top[a][:], ALU.subtract)
+            for a in which:
+                nc.vector.scalar_tensor_tensor(result[a][:], rest[a][:], 0.0, members[t][a][:, 0::2], ALU.min, ALU.add)
+                nc.sync.dma_start(out[P * t : P * (t + 1), halves[a]], result[a][:])
+
+        nc.vector.tensor_copy(h[0][:, :S], h_bank[0][:])
+        fetch(0)
+        for t in (1, 2):
+            nc.scalar.copy(h[t][:, :S], h_bank[t][:])
+            fetch(t)
+        finish(0, (0, 1))
+        nc.vector.tensor_copy(h[3][:, :S], h_bank[3][:])
+        fetch(3)
+        finish(1, (0, 1))
+        finish(2, (0, 1))
+        finish(3, (0,))
+        finish(3, (1,))

@@ -37,9 +37,9 @@ def tile_picked_jkeymixhopggpair_none_p_kernel(
             nc.sync.dma_start(t[:], src)
             return t
 
-        def mx_tiles(name, width):
-            words = keep.tile([P, width], U32, name=name + "_words", align_bytes=64)
-            scales = keep.tile([P, width], U8, name=name + "_scales", align_bytes=64)
+        def mx_tiles(name, width, words_tag="", scales_tag=""):
+            words = keep.tile([P, width], U32, name=name + "_words", tag=words_tag, align_bytes=64)
+            scales = keep.tile([P, width], U8, name=name + "_scales", tag=scales_tag, align_bytes=64)
             return words, scales
 
         def quantize(dst, src, cols):
@@ -64,42 +64,42 @@ def tile_picked_jkeymixhopggpair_none_p_kernel(
 
         x_tab = mx_tiles("x_tab", T)
         d_tab = mx_tiles("d_tab", G)
-        nc.vector.memset(d_tab[1][:].bitcast(I32), 0)
-        offs_t = load_list("offs_t", offs)
-        x_rows = x_scales[0].bitcast(I32).rearrange("(q r) c -> r q c", r=4)
-        for r in range(4):
-            nc.scalar.dma_start(x_tab[1][r:P:4, :].bitcast(I32), x_rows[r].unsqueeze(1).to_broadcast([4, 8, T // 4]))
-        nc.sync.dma_start(x_tab[0][:].bitcast(I32), x_words[0].rearrange("p n t -> p (n t)").bitcast(I32))
-        half = H // 2
-        w1_raw = [keep.tile([P, PACK, half], F32, name="w1_raw%d" % a) for a in range(2)]
-        for a in range(2):
-            nc.sync.dma_start(w1_raw[a][:], w1[:, half * a : half * (a + 1)].rearrange("(p j) c -> p j c", j=PACK))
-        two_t = load_list("two_t", two)
-        kidx_t = load_list("kidx_t", kidx)
+        nc.gpsimd.memset(d_tab[1][:].bitcast(I32), 0)
         d_rows = d_scales[0].bitcast(I32).rearrange("(g e) c -> e g c", e=2)
         for e in range(2):
-            nc.scalar.dma_start(d_tab[1][e:P:16, :].bitcast(I32), d_rows[e])
-        nc.sync.dma_start(d_tab[0][:].bitcast(I32), d_words[0].rearrange("p n t -> p (n t)").bitcast(I32))
+            nc.gpsimd.dma_start(d_tab[1][e:P:16, :].bitcast(I32), d_rows[e])
+        gn_t = keep.tile([P, PACK], F32, name="gn_t")
+        gk_t = keep.tile([P, PACK], F32, name="gk_t", tag="gk", align_bytes=64)
+        nc.gpsimd.dma_start(gn_t[:], gn.rearrange("(p t) o -> p (t o)", t=PACK))
+        nc.gpsimd.dma_start(gk_t[:], gk.rearrange("(p t) o -> p (t o)", t=PACK))
+        offs_t = load_list("offs_t", offs)
+        two_t = load_list("two_t", two)
+        x_rows = x_scales[0].bitcast(I32).rearrange("(q r) c -> r q c", r=4)
+        for r in range(4):
+            nc.sync.dma_start(x_tab[1][r:P:4, :].bitcast(I32), x_rows[r].unsqueeze(1).to_broadcast([4, 8, T // 4]))
+        nc.sync.dma_start(x_tab[0][:].bitcast(I32), x_words[0].rearrange("p n t -> p (n t)").bitcast(I32))
+        half = H // 2
+        w1_raw = [keep.tile([P, PACK, half], F32, name="w1_raw%d" % a, tag="w1_raw%d" % a, align_bytes=64) for a in range(2)]
+        for a in range(2):
+            nc.sync.dma_start(w1_raw[a][:], w1[:, half * a : half * (a + 1)].rearrange("(p j) c -> p j c", j=PACK))
         n1_t = load_list("n1_t", n1)
         n2_t = load_list("n2_t", n2)
         n3_t = load_list("n3_t", n3)
+        kidx_t = load_list("kidx_t", kidx)
+        nc.sync.dma_start(d_tab[0][:].bitcast(I32), d_words[0].rearrange("p n t -> p (n t)").bitcast(I32))
         n4_t = load_list("n4_t", n4)
         n5_t = load_list("n5_t", n5)
-        gn_t = keep.tile([P, PACK], F32, name="gn_t")
-        gk_t = keep.tile([P, PACK], F32, name="gk_t")
-        nc.sync.dma_start(gn_t[:], gn.rearrange("(p t) o -> p (t o)", t=PACK))
-        nc.sync.dma_start(gk_t[:], gk.rearrange("(p t) o -> p (t o)", t=PACK))
         w3_raw = keep.tile([P, PACK, N], F32, name="w3_raw")
         w2_raw = keep.tile([P, PACK, N], F32, name="w2_raw")
-        nc.sync.dma_start(w3_raw[:], w3.rearrange("(p j) c -> p j c", j=PACK))
         nc.sync.dma_start(w2_raw[:], w2.rearrange("(p j) c -> p j c", j=PACK))
+        nc.sync.dma_start(w3_raw[:], w3.rearrange("(p j) c -> p j c", j=PACK))
         n6_t = load_list("n6_t", n6)
 
         x_idx = mx_tiles("x_idx", S)
         nc.vector.tensor_copy(x_idx[1][:], x_tab[1][:].indirect(offs_t[:]))
         nc.vector.tensor_copy(x_idx[0][:], x_tab[0][:].indirect(offs_t[:]))
 
-        w1_bf = keep.tile([P, PACK * H], BF16, name="w1_bf", align_bytes=64)
+        w1_bf = keep.tile([P, PACK * H], BF16, name="w1_bf", tag="w1_bf", align_bytes=64)
         w1_view = w1_bf[:].rearrange("p (t m j) -> p m j t", t=PACK, j=PACK)
         for a in range(2):
             nc.scalar.copy(
@@ -118,7 +118,7 @@ def tile_picked_jkeymixhopggpair_none_p_kernel(
         for t in range(PACK):
             product(y_bank[t], w1_q, t, x_idx, True, True)
 
-        keys = mx_tiles("keys", H)
+        keys = mx_tiles("keys", H, "w1_bf", "w1_raw1")
         keys_dealt = mx_tiles("keys_dealt", H)
         keys_plane = keep.tile([P, H], U8, name="keys_plane", align_bytes=64)
         nc.vector.tensor_copy(keys[1][:], d_tab[1][:].indirect(kidx_t[:]))
@@ -138,7 +138,7 @@ def tile_picked_jkeymixhopggpair_none_p_kernel(
             product(s_bank[t], (keys_dealt[0], keys_plane), t, x_two, True, True)
 
         minus_gn = keep.tile([P, PACK], F32, name="minus_gn")
-        nc.vector.tensor_scalar(minus_gn[:], gn_t[:], -1.0, None, ALU.mult)
+        nc.gpsimd.tensor_scalar(minus_gn[:], gn_t[:], -1.0, 0.0, ALU.mult, ALU.add)
 
         halves = [slice(0, S // 2), slice(S // 2, S)]
         minus_d = keep.tile([P, PACK, S], F32, name="minus_d")
@@ -205,7 +205,7 @@ def tile_picked_jkeymixhopggpair_none_p_kernel(
                     raw[:, :, P * t : P * (t + 1)].rearrange("p j (c i) -> p c j i", i=4),
                 )
 
-        z_bf = keep.tile([P, PACK * S], BF16, name="z_bf", align_bytes=64)
+        z_bf = keep.tile([P, PACK * S], BF16, name="z_bf", tag="gk", align_bytes=64)
         z2_bf = keep.tile([P, PACK * S], BF16, name="z2_bf", align_bytes=64)
         z_q = mx_tiles("z_q", S)
         z2_q = mx_tiles("z2_q", S)
@@ -226,44 +226,51 @@ def tile_picked_jkeymixhopggpair_none_p_kernel(
         quantize(w_q, w_bf, slice(0, 2 * P))
         quantize(z2_q, z2_bf, halves[1])
         h_bank = [psum.tile([P, S], F32, name="y_bank%d" % t) for t in range(PACK)]
-        for t in range(PACK):
+
+        def h_product(t):
             if t > 0:
                 quantize(w_q, w_bf, slice(2 * P * t, 2 * P * (t + 1)))
             product(h_bank[t], w_q, 2 * t, z_q, True, False)
             product(h_bank[t], w_q, 2 * t + 1, z2_q, False, True)
 
         h = [keep.tile([P, NARROW], F32, name="h%d" % t) for t in range(PACK)]
-        members = [[keep.tile([P, S], F32, name="members%d_%d" % (t, a)) for a in range(2)] for t in range(PACK)]
+        members = [keep.tile([P, W], F32, name="members%d" % t) for t in range(PACK)]
+        pieces = [halves] * (PACK - 1) + [[halves[0], slice(S // 2, 3 * S // 4), slice(3 * S // 4, S)]]
 
-        def fetch(t):
-            for a in range(2):
-                window = h[t][:].indirect(n6_t[:, 32 * a : 32 * (a + 1)])
+        def fetch(t, group):
+            for cols in group:
+                window = h[t][:].indirect(n6_t[:, cols.start // 8 : cols.stop // 8])
+                dst = members[t][:, 2 * cols.start : 2 * cols.stop]
                 if t == 0:
-                    nc.vector.tensor_copy(members[t][a][:], window)
+                    nc.vector.tensor_copy(dst, window)
                 else:
-                    nc.scalar.activation(members[t][a][:], window, ACT.Copy)
+                    nc.scalar.activation(dst, window, ACT.Copy)
 
-        def finish(t, which):
-            top = {a: ring.tile([P, S // 2], F32, name="top") for a in which}
-            rest = {a: ring.tile([P, S // 2], F32, name="rest") for a in which}
-            result = {a: ring.tile([P, S // 2], F32, name="result") for a in which}
-            for a in which:
-                nc.vector.tensor_tensor(top[a][:], h[t][:, halves[a]], members[t][a][:, 0::2], ALU.max)
-            for a in which:
-                nc.vector.tensor_tensor(rest[a][:], members[t][a][:, 1::2], top[a][:], ALU.subtract)
-            for a in which:
-                nc.vector.scalar_tensor_tensor(result[a][:], rest[a][:], 0.0, members[t][a][:, 0::2], ALU.min, ALU.add)
-                nc.sync.dma_start(out[P * t : P * (t + 1), halves[a]], result[a][:])
+        def finish(t, group):
+            top = [ring.tile([P, c.stop - c.start], F32, name="top") for c in group]
+            rest = [ring.tile([P, c.stop - c.start], F32, name="rest") for c in group]
+            result = [ring.tile([P, c.stop - c.start], F32, name="result") for c in group]
+            first = [members[t][:, 2 * c.start : 2 * c.stop : 2] for c in group]
+            second = [members[t][:, 2 * c.start + 1 : 2 * c.stop : 2] for c in group]
+            for a, cols in enumerate(group):
+                nc.vector.tensor_tensor(top[a][:], h[t][:, cols], first[a], ALU.max)
+            for a, cols in enumerate(group):
+                nc.vector.tensor_tensor(rest[a][:], second[a], top[a][:], ALU.subtract)
+            for a, cols in enumerate(group):
+                nc.vector.scalar_tensor_tensor(result[a][:], rest[a][:], 0.0, first[a], ALU.min, ALU.add)
+                nc.sync.dma_start(out[P * t : P * (t + 1), cols], result[a][:])
 
+        h_product(0)
+        h_product(1)
         nc.vector.tensor_copy(h[0][:, :S], h_bank[0][:])
-        fetch(0)
-        for t in (1, 2):
+        h_product(2)
+        fetch(0, pieces[0][:1])
+        h_product(3)
+        fetch(0, pieces[0][1:])
+        for t in range(1, PACK):
             nc.scalar.copy(h[t][:, :S], h_bank[t][:])
-            fetch(t)
-        finish(0, (0, 1))
-        nc.vector.tensor_copy(h[3][:, :S], h_bank[3][:])
-        fetch(3)
-        finish(1, (0, 1))
-        finish(2, (0, 1))
-        finish(3, (0,))
-        finish(3, (1,))
+            fetch(t, pieces[t])
+        for t in range(PACK - 1):
+            finish(t, pieces[t])
+        for cols in pieces[3]:
+            finish(3, [cols])

@@ -19,7 +19,7 @@ P = 128
 PACK = 4
 WIDE = 2 * S
 NARROW = S + 16
-FUSED_TILES = (0, 1, 2)
+FUSED_LOOKUPS = 5
 
 
 def tile_picked_jkeymixhopggpair_none_p_kernel(
@@ -68,10 +68,6 @@ def tile_picked_jkeymixhopggpair_none_p_kernel(
         d_rows = d_scales[0].bitcast(I32).rearrange("(g e) c -> e g c", e=2)
         for e in range(2):
             nc.gpsimd.dma_start(d_tab[1][e:P:16, :].bitcast(I32), d_rows[e])
-        gn_t = keep.tile([P, PACK], F32, name="gn_t")
-        gk_t = keep.tile([P, PACK], F32, name="gk_t", tag="gk", align_bytes=64)
-        nc.gpsimd.dma_start(gn_t[:], gn.rearrange("(p t) o -> p (t o)", t=PACK))
-        nc.gpsimd.dma_start(gk_t[:], gk.rearrange("(p t) o -> p (t o)", t=PACK))
         offs_t = load_list("offs_t", offs)
         two_t = load_list("two_t", two)
         x_rows = x_scales[0].bitcast(I32).rearrange("(q r) c -> r q c", r=4)
@@ -89,11 +85,22 @@ def tile_picked_jkeymixhopggpair_none_p_kernel(
         nc.sync.dma_start(d_tab[0][:].bitcast(I32), d_words[0].rearrange("p n t -> p (n t)").bitcast(I32))
         n4_t = load_list("n4_t", n4)
         n5_t = load_list("n5_t", n5)
-        w3_raw = keep.tile([P, PACK, N], F32, name="w3_raw")
-        w2_raw = keep.tile([P, PACK, N], F32, name="w2_raw")
-        nc.sync.dma_start(w2_raw[:], w2.rearrange("(p j) c -> p j c", j=PACK))
-        nc.sync.dma_start(w3_raw[:], w3.rearrange("(p j) c -> p j c", j=PACK))
+        gn_t = keep.tile([P, PACK], F32, name="gn_t")
+        gk_t = [keep.tile([P, 1], F32, name="gk%d" % t, tag="gk%d" % t, align_bytes=64) for t in range(PACK)]
+        nc.sync.dma_start(gn_t[:], gn.rearrange("(p t) o -> p (t o)", t=PACK))
+        w_raw = keep.tile([P, 2, PACK, N], F32, name="w_raw")
+        nc.sync.dma_start(w_raw[:, 0], w2.rearrange("(p j) c -> p j c", j=PACK))
+        w3_rows = w3.rearrange("(b t i) c -> t b i c", t=PACK, i=8)
+        for t in range(PACK):
+            nc.sync.dma_start(w_raw[:, 1, t, :], w3_rows[t])
+        with nc.allow_non_contiguous_dma(reason="one gain a partition and slot"):
+            for t in range(PACK):
+                nc.sync.dma_start(gk_t[t][:], gk.rearrange("(b t i) o -> t b i o", t=PACK, i=8)[t])
         n6_t = load_list("n6_t", n6)
+
+        warm = keep.tile([P, 2], F32, name="warm")
+        nc.gpsimd.memset(warm[:, 0:1], 0.0)
+        nc.scalar.activation(warm[:, 1:2], warm[:, 0:1], ACT.Sigmoid)
 
         x_idx = mx_tiles("x_idx", S)
         nc.vector.tensor_copy(x_idx[1][:], x_tab[1][:].indirect(offs_t[:]))
@@ -123,14 +130,15 @@ def tile_picked_jkeymixhopggpair_none_p_kernel(
         keys_plane = keep.tile([P, H], U8, name="keys_plane", align_bytes=64)
         nc.vector.tensor_copy(keys[1][:], d_tab[1][:].indirect(kidx_t[:]))
         nc.vector.tensor_copy(keys[0][:], d_tab[0][:].indirect(kidx_t[:]))
+        for dst in (keys_dealt[1], keys_plane):
+            nc.vector.tensor_copy(
+                dst[:].bitcast(I32).rearrange("p (t b i) -> p t b i", t=PACK, i=2),
+                keys[1][:].bitcast(I32).rearrange("p (b t i) -> p t b i", t=PACK, i=2),
+            )
         nc.vector.tensor_copy(
-            keys_dealt[1][:].rearrange("p (t m) -> p m t", t=PACK), keys[1][:].rearrange("p (m t) -> p m t", t=PACK)
+            keys_dealt[0][:].bitcast(I32).rearrange("p (t b i) -> p t b i", t=PACK, i=8),
+            keys[0][:].bitcast(I32).rearrange("p (b t i) -> p t b i", t=PACK, i=8),
         )
-        nc.vector.tensor_copy(
-            keys_dealt[0][:].bitcast(I32).rearrange("p (t c i) -> p c t i", t=PACK, i=4),
-            keys[0][:].bitcast(I32).rearrange("p (c i t) -> p c t i", t=PACK, i=4),
-        )
-        nc.vector.tensor_copy(keys_plane[:].bitcast(I32), keys_dealt[1][:].bitcast(I32))
         for e in range(2):
             nc.sync.dma_start(keys_plane[2 + e : P : 32, :].bitcast(I32), keys_dealt[1][16 + e : P : 32, :].bitcast(I32))
         s_bank = [psum.tile([P, S], F32, name="s_bank%d" % t) for t in range(PACK)]
@@ -153,39 +161,77 @@ def tile_picked_jkeymixhopggpair_none_p_kernel(
             s.append(keep.tile([P, WIDE], F32, name="s%d" % t, tag="s%d" % t, align_bytes=64))
             gate.append(keep.tile([P, S], F32, name="gate%d" % t, tag="gate%d" % t))
 
+        lookups = [(t, dst, lst) for t in range(PACK) for dst, lst in ((y_n2, n2_t), (y_n3, n3_t))]
+        fused, plain = lookups[:FUSED_LOOKUPS], lookups[FUSED_LOOKUPS:]
+        nc.scalar.copy(y[0][:, :S], y_bank[0][:])
         for t in range(PACK):
-            nc.scalar.copy(y[t][:, :S], y_bank[t][:])
+            if t + 1 < PACK:
+                nc.scalar.copy(y[t + 1][:, :S], y_bank[t + 1][:])
             nc.scalar.activation(y_n1[t][:], y[t][:].indirect(n1_t[:]), ACT.Copy)
-            if t not in FUSED_TILES:
-                nc.scalar.activation(y_n2[t][:], y[t][:].indirect(n2_t[:]), ACT.Copy)
-                nc.scalar.activation(y_n3[t][:], y[t][:].indirect(n3_t[:]), ACT.Copy)
+        for t, dst, lst in plain:
+            nc.scalar.activation(dst[t][:], y[t][:].indirect(lst[:]), ACT.Copy)
+        nc.scalar.activation(s[0][:, :S], s_bank[0][:], ACT.Copy, scale=0.0625)
         for t in range(PACK):
-            nc.scalar.activation(s[t][:, :S], s_bank[t][:], ACT.Copy, scale=0.0625)
+            if t + 1 < PACK:
+                nc.scalar.activation(s[t + 1][:, :S], s_bank[t + 1][:], ACT.Copy, scale=0.0625)
             nc.scalar.activation(gate[t][:], s[t][:].indirect(n4_t[:]), ACT.Sigmoid)
 
         def left_step(t):
             nc.vector.tensor_tensor(left[t][:], y[t][:, :S], y_n1[t][:], ALU.max)
 
         def st_step(t):
-            nc.vector.scalar_tensor_tensor(st[:, t, :S], s[t][:, :S], gk_t[:, t : t + 1], gate[t][:], ALU.mult, ALU.mult)
+            nc.vector.scalar_tensor_tensor(st[:, t, :S], s[t][:, :S], gk_t[t][:], gate[t][:], ALU.mult, ALU.mult)
+
+        w_bf_first = keep.tile([P, 2 * PACK * P], BF16, name="w_bf_first", align_bytes=64)
+
+        def cast_w(t, copy, dst):
+            copy(
+                dst.rearrange("p (b c i j) -> p b c j i", b=2, i=4, j=PACK),
+                w_raw[:, :, :, P * t : P * (t + 1)].rearrange("p b j (c i) -> p b c j i", i=4),
+            )
+
+        def fused_step(t, dst, lst):
+            nc.vector.tensor_tensor(dst[t][:], y[t][:].indirect(lst[:]), left[t][:], ALU.subtract)
 
         left_step(0)
-        for t in FUSED_TILES:
-            nc.vector.tensor_tensor(y_n2[t][:], y[t][:].indirect(n2_t[:]), left[t][:], ALU.subtract)
-            nc.vector.tensor_tensor(y_n3[t][:], y[t][:].indirect(n3_t[:]), left[t][:], ALU.subtract)
+        for t in range(2):
+            fused_step(t, y_n2, n2_t)
+            fused_step(t, y_n3, n3_t)
             left_step(t + 1)
             nc.vector.tensor_tensor(minus_d[:, t, :], y_n2[t][:], y_n3[t][:], ALU.max)
-        done = 0
-        for t in range(len(FUSED_TILES), PACK):
-            right = ring.tile([P, S], F32, name="right")
-            nc.vector.tensor_tensor(right[:], y_n2[t][:], y_n3[t][:], ALU.max)
-            st_step(done)
-            done += 1
-            nc.vector.tensor_tensor(minus_d[:, t, :], right[:], left[t][:], ALU.subtract)
-            if t + 1 < PACK:
-                left_step(t + 1)
-        for t in range(done, PACK):
-            st_step(t)
+            if t == 0:
+                cast_w(0, nc.vector.tensor_copy, w_bf_first[:])
+        fused_step(2, y_n2, n2_t)
+        left_step(3)
+        over = keep.tile([P, S], F32, name="over")
+        right = keep.tile([P, S], F32, name="right")
+        nc.vector.tensor_tensor(over[:], y_n3[2][:], left[2][:], ALU.subtract)
+        nc.vector.tensor_tensor(right[:], y_n2[3][:], y_n3[3][:], ALU.max)
+        nc.vector.tensor_tensor(minus_d[:, 2, :], y_n2[2][:], over[:], ALU.max)
+        st_step(0)
+        nc.vector.tensor_tensor(minus_d[:, 3, :], right[:], left[3][:], ALU.subtract)
+        st_step(1)
+        st_step(2)
+
+        z_bf = [keep.tile([P, PACK * S // 2], BF16, name="z_bf%d" % a, tag="gk%d" % (2 + a), align_bytes=64) for a in range(2)]
+        z2_bf = [keep.tile([P, PACK * S // 2], BF16, name="z2_bf%d" % a, align_bytes=64) for a in range(2)]
+        z_q = mx_tiles("z_q", S)
+        z2_q = mx_tiles("z2_q", S)
+        w_q = mx_tiles("w_q", 2 * N)
+
+        def woven(bf):
+            return bf[:].rearrange("p (c i t) -> p c t i", i=4, t=PACK)
+
+        def planes(src):
+            return src.rearrange("p t (c i) -> p c t i", i=4)
+
+        def quantize_part(dst, cols, src):
+            nc.vector.quantize_mx(out=dst[0][:, cols].bitcast(FP8X4), scales=dst[1][:, cols], in_=src)
+
+        gain = minus_gn[:].unsqueeze(1).unsqueeze(3).to_broadcast([P, S // 8, PACK, 4])
+        nc.vector.tensor_tensor(woven(z_bf[0]), planes(minus_d[:, :, halves[0]]), gain, ALU.mult)
+        st_step(3)
+        nc.vector.tensor_tensor(woven(z_bf[1]), planes(minus_d[:, :, halves[1]]), gain, ALU.mult)
 
         st_n5 = [
             keep.tile([P, PACK, S // 2], F32, name="st_n5_0"),
@@ -195,47 +241,32 @@ def tile_picked_jkeymixhopggpair_none_p_kernel(
             for t in range(PACK):
                 nc.scalar.activation(st_n5[a][:, t, :], st[:, t, :].indirect(n5_t[:, 16 * a : 16 * (a + 1)]), ACT.Copy)
 
-        w_bf = keep.tile([P, PACK * 2 * PACK * P], BF16, name="w_bf", tag="s3", align_bytes=64)
-        w_q = mx_tiles("w_q", 2 * N)
-        for t in range(PACK):
-            for b, raw in enumerate((w2_raw, w3_raw)):
-                at = PACK * P * (2 * t + b)
-                nc.scalar.copy(
-                    w_bf[:, at : at + PACK * P].rearrange("p (c i j) -> p c j i", i=4, j=PACK),
-                    raw[:, :, P * t : P * (t + 1)].rearrange("p j (c i) -> p c j i", i=4),
-                )
+        w_bf_rest = keep.tile([P, 3 * 2 * PACK * P], BF16, name="w_bf_rest", tag="s3", align_bytes=64)
+        w_bf = [w_bf_first[:]] + [w_bf_rest[:, 2 * PACK * P * a : 2 * PACK * P * (a + 1)] for a in range(3)]
+        for t in range(1, PACK):
+            cast_w(t, nc.scalar.copy, w_bf[t])
 
-        z_bf = keep.tile([P, PACK * S], BF16, name="z_bf", tag="gk", align_bytes=64)
-        z2_bf = keep.tile([P, PACK * S], BF16, name="z2_bf", align_bytes=64)
-        z_q = mx_tiles("z_q", S)
-        z2_q = mx_tiles("z2_q", S)
+        def quantize_w(t):
+            quantize_part(w_q, slice(2 * P * t, 2 * P * (t + 1)), w_bf[t])
 
-        def woven(bf, cols):
-            return bf[:, PACK * cols.start : PACK * cols.stop].rearrange("p (c i t) -> p c t i", i=4, t=PACK)
-
-        def planes(src):
-            return src.rearrange("p t (c i) -> p c t i", i=4)
-
-        gain = minus_gn[:].unsqueeze(1).unsqueeze(3).to_broadcast([P, S // 8, PACK, 4])
-        for cols in halves:
-            nc.vector.tensor_tensor(woven(z_bf, cols), planes(minus_d[:, :, cols]), gain, ALU.mult)
-        nc.vector.tensor_tensor(woven(z2_bf, halves[0]), planes(st[:, :, halves[0]]), planes(st_n5[0][:]), ALU.subtract)
-        quantize(z_q, z_bf, slice(0, S))
-        nc.vector.tensor_tensor(woven(z2_bf, halves[1]), planes(st[:, :, halves[1]]), planes(st_n5[1][:]), ALU.subtract)
-        quantize(z2_q, z2_bf, halves[0])
-        quantize(w_q, w_bf, slice(0, 2 * P))
-        quantize(z2_q, z2_bf, halves[1])
+        quantize_part(z_q, halves[0], z_bf[0][:])
+        quantize_w(0)
+        quantize_part(z_q, halves[1], z_bf[1][:])
+        for a in range(2):
+            nc.vector.tensor_tensor(woven(z2_bf[a]), planes(st[:, :, halves[a]]), planes(st_n5[a][:]), ALU.subtract)
+        quantize_part(z2_q, halves[0], z2_bf[0][:])
+        quantize_part(z2_q, halves[1], z2_bf[1][:])
         h_bank = [psum.tile([P, S], F32, name="y_bank%d" % t) for t in range(PACK)]
 
         def h_product(t):
             if t > 0:
-                quantize(w_q, w_bf, slice(2 * P * t, 2 * P * (t + 1)))
+                quantize_w(t)
             product(h_bank[t], w_q, 2 * t, z_q, True, False)
             product(h_bank[t], w_q, 2 * t + 1, z2_q, False, True)
 
         h = [keep.tile([P, NARROW], F32, name="h%d" % t) for t in range(PACK)]
         members = [keep.tile([P, W], F32, name="members%d" % t) for t in range(PACK)]
-        pieces = [halves] * (PACK - 1) + [[halves[0], slice(S // 2, 3 * S // 4), slice(3 * S // 4, S)]]
+        pieces = [halves] * PACK
 
         def fetch(t, group):
             for cols in group:
@@ -262,15 +293,15 @@ def tile_picked_jkeymixhopggpair_none_p_kernel(
 
         h_product(0)
         h_product(1)
-        nc.vector.tensor_copy(h[0][:, :S], h_bank[0][:])
         h_product(2)
-        fetch(0, pieces[0][:1])
+        nc.vector.tensor_copy(h[0][:, :S], h_bank[0][:])
         h_product(3)
-        fetch(0, pieces[0][1:])
+        fetch(0, halves)
+        nc.scalar.copy(h[1][:, :S], h_bank[1][:])
         for t in range(1, PACK):
-            nc.scalar.copy(h[t][:, :S], h_bank[t][:])
-            fetch(t, pieces[t])
-        for t in range(PACK - 1):
-            finish(t, pieces[t])
-        for cols in pieces[3]:
-            finish(3, [cols])
+            fetch(t, halves[:1])
+            if t + 1 < PACK:
+                nc.scalar.copy(h[t + 1][:, :S], h_bank[t + 1][:])
+            fetch(t, halves[1:])
+        for t in range(PACK):
+            finish(t, halves)

@@ -50,14 +50,14 @@ def tile_picked_jkeymixhopggpair_none_p_kernel(
                 in_=src[:, PACK * cols.start : PACK * cols.stop],
             )
 
-        def product(acc, lhs, tile_index, rhs, start, stop):
+        def product(acc, lhs, tile_index, rhs, start, stop, places=slice(0, S)):
             cols = slice(P * tile_index, P * (tile_index + 1))
             nc.tensor.matmul_mx(
-                out=acc[:],
+                out=acc[:, places],
                 lhsT=lhs[0][:, cols].bitcast(FP8X4),
                 lhsT_scale=lhs[1][:, cols],
-                rhs=rhs[0][:].bitcast(FP8X4),
-                rhs_scale=rhs[1][:],
+                rhs=rhs[0][:, places].bitcast(FP8X4),
+                rhs_scale=rhs[1][:, places],
                 start=start,
                 stop=stop,
             )
@@ -73,11 +73,11 @@ def tile_picked_jkeymixhopggpair_none_p_kernel(
         x_rows = x_scales[0].bitcast(I32).rearrange("(q r) c -> r q c", r=4)
         for r in range(4):
             nc.sync.dma_start(x_tab[1][r:P:4, :].bitcast(I32), x_rows[r].unsqueeze(1).to_broadcast([4, 8, T // 4]))
-        nc.sync.dma_start(x_tab[0][:].bitcast(I32), x_words[0].rearrange("p n t -> p (n t)").bitcast(I32))
+        nc.scalar.dma_start(x_tab[0][:].bitcast(I32), x_words[0].rearrange("p n t -> p (n t)").bitcast(I32))
         half = H // 2
         w1_raw = [keep.tile([P, PACK, half], F32, name="w1_raw%d" % a, tag="w1_raw%d" % a, align_bytes=64) for a in range(2)]
         for a in range(2):
-            nc.sync.dma_start(w1_raw[a][:], w1[:, half * a : half * (a + 1)].rearrange("(p j) c -> p j c", j=PACK))
+            (nc.scalar if a == 0 else nc.sync).dma_start(w1_raw[a][:], w1[:, half * a : half * (a + 1)].rearrange("(p j) c -> p j c", j=PACK))
         n1_t = load_list("n1_t", n1)
         n2_t = load_list("n2_t", n2)
         n3_t = load_list("n3_t", n3)
@@ -249,20 +249,28 @@ def tile_picked_jkeymixhopggpair_none_p_kernel(
         def quantize_w(t):
             quantize_part(w_q, slice(2 * P * t, 2 * P * (t + 1)), w_bf[t])
 
+        def z2_step(a):
+            nc.vector.tensor_tensor(woven(z2_bf[a]), planes(st[:, :, halves[a]]), planes(st_n5[a][:]), ALU.subtract)
+
         quantize_part(z_q, halves[0], z_bf[0][:])
         quantize_w(0)
+        z2_step(0)
         quantize_part(z_q, halves[1], z_bf[1][:])
-        for a in range(2):
-            nc.vector.tensor_tensor(woven(z2_bf[a]), planes(st[:, :, halves[a]]), planes(st_n5[a][:]), ALU.subtract)
         quantize_part(z2_q, halves[0], z2_bf[0][:])
+        z2_step(1)
+        quantize_w(1)
         quantize_part(z2_q, halves[1], z2_bf[1][:])
         h_bank = [psum.tile([P, S], F32, name="y_bank%d" % t) for t in range(PACK)]
 
         def h_product(t):
-            if t > 0:
+            if t > 1:
                 quantize_w(t)
             product(h_bank[t], w_q, 2 * t, z_q, True, False)
-            product(h_bank[t], w_q, 2 * t + 1, z2_q, False, True)
+            if t == 0:
+                product(h_bank[t], w_q, 1, z2_q, False, False, halves[0])
+                product(h_bank[t], w_q, 1, z2_q, False, True, halves[1])
+            else:
+                product(h_bank[t], w_q, 2 * t + 1, z2_q, False, True)
 
         h = [keep.tile([P, NARROW], F32, name="h%d" % t) for t in range(PACK)]
         members = [keep.tile([P, W], F32, name="members%d" % t) for t in range(PACK)]

from contextlib import ExitStack

import concourse.mybir as mybir

K, T, S, N, H, G, W = 512, 1024, 512, 512, 512, 2048, 1024
FLOPS = 4 * 2 * 512 * 512 * 512

F32 = mybir.dt.float32
BF16 = mybir.dt.bfloat16
I32 = mybir.dt.int32
U32 = mybir.dt.uint32
U16 = mybir.dt.uint16
U8 = mybir.dt.uint8
FP8X4 = mybir.dt.float8_e4m3fn_x4
ALU = mybir.AluOpType
ACT = mybir.ActivationFunctionType

P = 128
PACK = 4
WIDE = 2 * S
NARROW = S + 16
FUSED_LOOKUPS = 5


def tile_picked_jkeymixhopggpair_none_p_kernel(
    tc, x_words, x_scales, w1, d_words, d_scales, gn, gk, w2, w3, offs, kidx, two, n1, n2, n3, n4, n5, n6, out
):
    nc = tc.nc
    with ExitStack() as ctx:
        lists = ctx.enter_context(tc.tile_pool(name="lists", bufs=1))
        keep = ctx.enter_context(tc.tile_pool(name="keep", bufs=1))
        ring = ctx.enter_context(tc.tile_pool(name="ring", bufs=4))
        psum = ctx.enter_context(tc.psum_pool(name="psum", bufs=1))

        def load_list(name, src):
            t = lists.tile(list(src.shape), U16, name=name)
            nc.sync.dma_start(t[:], src)
            return t

        def mx_tiles(name, width, words_tag="", scales_tag=""):
            words = keep.tile([P, width], U32, name=name + "_words", tag=words_tag, align_bytes=64)
            scales = keep.tile([P, width], U8, name=name + "_scales", tag=scales_tag, align_bytes=64)
            return words, scales

        def quantize(dst, src, cols):
            words, scales = dst
            nc.vector.quantize_mx(
                out=words[:, cols].bitcast(FP8X4),
                scales=scales[:, cols],
                in_=src[:, PACK * cols.start : PACK * cols.stop],
            )

        def product(acc, lhs, tile_index, rhs, start, stop, places=slice(0, S)):
            cols = slice(P * tile_index, P * (tile_index + 1))
            nc.tensor.matmul_mx(
                out=acc[:, places],
                lhsT=lhs[0][:, cols].bitcast(FP8X4),
                lhsT_scale=lhs[1][:, cols],
                rhs=rhs[0][:, places].bitcast(FP8X4),
                rhs_scale=rhs[1][:, places],
                start=start,
                stop=stop,
            )

        x_tab = mx_tiles("x_tab", T)
        d_tab = mx_tiles("d_tab", G)
        nc.gpsimd.memset(d_tab[1][:].bitcast(I32), 0)
        d_rows = d_scales[0].bitcast(I32).rearrange("(g e) c -> e g c", e=2)
        for e in range(2):
            nc.gpsimd.dma_start(d_tab[1][e:P:16, :].bitcast(I32), d_rows[e])
        offs_t = load_list("offs_t", offs)
        two_t = load_list("two_t", two)
        x_rows = x_scales[0].bitcast(I32).rearrange("(q r) c -> r q c", r=4)
        for r in range(4):
            nc.sync.dma_start(x_tab[1][r:P:4, :].bitcast(I32), x_rows[r].unsqueeze(1).to_broadcast([4, 8, T // 4]))
        nc.scalar.dma_start(x_tab[0][:].bitcast(I32), x_words[0].rearrange("p n t -> p (n t)").bitcast(I32))
        half = H // 2
        w1_raw = [keep.tile([P, PACK, half], F32, name="w1_raw%d" % a, tag="w1_raw%d" % a, align_bytes=64) for a in range(2)]
        for a in range(2):
            (nc.scalar if a == 0 else nc.sync).dma_start(w1_raw[a][:], w1[:, half * a : half * (a + 1)].rearrange("(p j) c -> p j c", j=PACK))
        n1_t = load_list("n1_t", n1)
        n2_t = load_list("n2_t", n2)
        n3_t = load_list("n3_t", n3)
        kidx_t = load_list("kidx_t", kidx)
        nc.sync.dma_start(d_tab[0][:].bitcast(I32), d_words[0].rearrange("p n t -> p (n t)").bitcast(I32))
        n4_t = load_list("n4_t", n4)
        n5_t = load_list("n5_t", n5)
        gn_t = keep.tile([P, PACK], F32, name="gn_t")
        gk_t = [keep.tile([P, 1], F32, name="gk%d" % t, tag="gk%d" % t, align_bytes=64) for t in range(PACK)]
        nc.sync.dma_start(gn_t[:], gn.rearrange("(p t) o -> p (t o)", t=PACK))
        w_raw = keep.tile([P, 2, PACK, N], F32, name="w_raw")
        nc.sync.dma_start(w_raw[:, 0], w2.rearrange("(p j) c -> p j c", j=PACK))
        w3_rows = w3.rearrange("(b t i) c -> t b i c", t=PACK, i=8)
        for t in range(PACK):
            nc.sync.dma_start(w_raw[:, 1, t, :], w3_rows[t])
        with nc.allow_non_contiguous_dma(reason="one gain a partition and slot"):
            for t in range(PACK):
                nc.sync.dma_start(gk_t[t][:], gk.rearrange("(b t i) o -> t b i o", t=PACK, i=8)[t])
        n6_t = load_list("n6_t", n6)

        warm = keep.tile([P, 2], F32, name="warm")
        nc.gpsimd.memset(warm[:, 0:1], 0.0)
        nc.scalar.activation(warm[:, 1:2], warm[:, 0:1], ACT.Sigmoid)

        x_idx = mx_tiles("x_idx", S)
        nc.vector.tensor_copy(x_idx[1][:], x_tab[1][:].indirect(offs_t[:]))
        nc.vector.tensor_copy(x_idx[0][:], x_tab[0][:].indirect(offs_t[:]))

        w1_bf = keep.tile([P, PACK * H], BF16, name="w1_bf", tag="w1_bf", align_bytes=64)
        w1_view = w1_bf[:].rearrange("p (t m j) -> p m j t", t=PACK, j=PACK)
        for a in range(2):
            nc.scalar.copy(
                w1_view[:, (P // 2) * a : (P // 2) * (a + 1)],
                w1_raw[a][:].rearrange("p j (m t) -> p m j t", t=PACK),
            )

        x_two = mx_tiles("x_two", S)
        nc.vector.tensor_copy(x_two[0][:], x_tab[0][:].indirect(two_t[:]))
        nc.vector.tensor_copy(x_two[1][:], x_tab[1][:].indirect(two_t[:]))
        w1_q = mx_tiles("w1_q", H)
        quantize(w1_q, w1_bf, slice(0, P))
        quantize(w1_q, w1_bf, slice(P, 2 * P))
        quantize(w1_q, w1_bf, slice(2 * P, 4 * P))
        y_bank = [psum.tile([P, S], F32, name="y_bank%d" % t) for t in range(PACK)]
        for t in range(PACK):
            product(y_bank[t], w1_q, t, x_idx, True, True)

        keys = mx_tiles("keys", H, "w1_bf", "w1_raw1")
        keys_dealt = mx_tiles("keys_dealt", H)
        keys_plane = keep.tile([P, H], U8, name="keys_plane", align_bytes=64)
        nc.vector.tensor_copy(keys[1][:], d_tab[1][:].indirect(kidx_t[:]))
        nc.vector.tensor_copy(keys[0][:], d_tab[0][:].indirect(kidx_t[:]))
        for dst in (keys_dealt[1], keys_plane):
            nc.vector.tensor_copy(
                dst[:].bitcast(I32).rearrange("p (t b i) -> p t b i", t=PACK, i=2),
                keys[1][:].bitcast(I32).rearrange("p (b t i) -> p t b i", t=PACK, i=2),
            )
        nc.vector.tensor_copy(
            keys_dealt[0][:].bitcast(I32).rearrange("p (t b i) -> p t b i", t=PACK, i=8),
            keys[0][:].bitcast(I32).rearrange("p (b t i) -> p t b i", t=PACK, i=8),
        )
        for e in range(2):
            nc.sync.dma_start(keys_plane[2 + e : P : 32, :].bitcast(I32), keys_dealt[1][16 + e : P : 32, :].bitcast(I32))
        s_bank = [psum.tile([P, S], F32, name="s_bank%d" % t) for t in range(PACK)]
        for t in range(PACK):
            product(s_bank[t], (keys_dealt[0], keys_plane), t, x_two, True, True)

        minus_gn = keep.tile([P, PACK], F32, name="minus_gn")
        nc.gpsimd.tensor_scalar(minus_gn[:], gn_t[:], -1.0, 0.0, ALU.mult, ALU.add)

        halves = [slice(0, S // 2), slice(S // 2, S)]
        minus_d = keep.tile([P, PACK, S], F32, name="minus_d")
        st = keep.tile([P, PACK, WIDE], F32, name="st")
        y, y_n1, left, y_n2, y_n3, s, gate = [], [], [], [], [], [], []
        for t in range(PACK):
            y.append(keep.tile([P, WIDE], F32, name="y%d" % t))
            y_n1.append(keep.tile([P, S], F32, name="y_n1_%d" % t))
            left.append(keep.tile([P, S], F32, name="left%d" % t))
            y_n2.append(keep.tile([P, S], F32, name="y_n2_%d" % t))
            y_n3.append(keep.tile([P, S], F32, name="y_n3_%d" % t))
            s.append(keep.tile([P, WIDE], F32, name="s%d" % t, tag="s%d" % t, align_bytes=64))
            gate.append(keep.tile([P, S], F32, name="gate%d" % t, tag="gate%d" % t))

        lookups = [(t, dst, lst) for t in range(PACK) for dst, lst in ((y_n2, n2_t), (y_n3, n3_t))]
        fused, plain = lookups[:FUSED_LOOKUPS], lookups[FUSED_LOOKUPS:]
        nc.scalar.copy(y[0][:, :S], y_bank[0][:])
        for t in range(PACK):
            if t + 1 < PACK:
                nc.scalar.copy(y[t + 1][:, :S], y_bank[t + 1][:])
            nc.scalar.activation(y_n1[t][:], y[t][:].indirect(n1_t[:]), ACT.Copy)
        for t, dst, lst in plain:
            nc.scalar.activation(dst[t][:], y[t][:].indirect(lst[:]), ACT.Copy)
        nc.scalar.activation(s[0][:, :S], s_bank[0][:], ACT.Copy, scale=0.0625)
        for t in range(PACK):
            if t + 1 < PACK:
                nc.scalar.activation(s[t + 1][:, :S], s_bank[t + 1][:], ACT.Copy, scale=0.0625)
            nc.scalar.activation(gate[t][:], s[t][:].indirect(n4_t[:]), ACT.Sigmoid)

        def left_step(t):
            nc.vector.tensor_tensor(left[t][:], y[t][:, :S], y_n1[t][:], ALU.max)

        def st_step(t):
            nc.vector.scalar_tensor_tensor(st[:, t, :S], s[t][:, :S], gk_t[t][:], gate[t][:], ALU.mult, ALU.mult)

        w_bf_first = keep.tile([P, 2 * PACK * P], BF16, name="w_bf_first", align_bytes=64)

        def cast_w(t, copy, dst):
            copy(
                dst.rearrange("p (b c i j) -> p b c j i", b=2, i=4, j=PACK),
                w_raw[:, :, :, P * t : P * (t + 1)].rearrange("p b j (c i) -> p b c j i", i=4),
            )

        def fused_step(t, dst, lst):
            nc.vector.tensor_tensor(dst[t][:], y[t][:].indirect(lst[:]), left[t][:], ALU.subtract)

        left_step(0)
        for t in range(2):
            fused_step(t, y_n2, n2_t)
            fused_step(t, y_n3, n3_t)
            left_step(t + 1)
            nc.vector.tensor_tensor(minus_d[:, t, :], y_n2[t][:], y_n3[t][:], ALU.max)
            if t == 0:
                cast_w(0, nc.vector.tensor_copy, w_bf_first[:])
        fused_step(2, y_n2, n2_t)
        left_step(3)
        over = keep.tile([P, S], F32, name="over")
        right = keep.tile([P, S], F32, name="right")
        nc.vector.tensor_tensor(over[:], y_n3[2][:], left[2][:], ALU.subtract)
        nc.vector.tensor_tensor(right[:], y_n2[3][:], y_n3[3][:], ALU.max)
        nc.vector.tensor_tensor(minus_d[:, 2, :], y_n2[2][:], over[:], ALU.max)
        st_step(0)
        nc.vector.tensor_tensor(minus_d[:, 3, :], right[:], left[3][:], ALU.subtract)
        st_step(1)
        st_step(2)

        z_bf = [keep.tile([P, PACK * S // 2], BF16, name="z_bf%d" % a, tag="gk%d" % (2 + a), align_bytes=64) for a in range(2)]
        z2_bf = [keep.tile([P, PACK * S // 2], BF16, name="z2_bf%d" % a, align_bytes=64) for a in range(2)]
        z_q = mx_tiles("z_q", S)
        z2_q = mx_tiles("z2_q", S)
        w_q = mx_tiles("w_q", 2 * N)

        def woven(bf):
            return bf[:].rearrange("p (c i t) -> p c t i", i=4, t=PACK)

        def planes(src):
            return src.rearrange("p t (c i) -> p c t i", i=4)

        def quantize_part(dst, cols, src):
            nc.vector.quantize_mx(out=dst[0][:, cols].bitcast(FP8X4), scales=dst[1][:, cols], in_=src)

        gain = minus_gn[:].unsqueeze(1).unsqueeze(3).to_broadcast([P, S // 8, PACK, 4])
        nc.vector.tensor_tensor(woven(z_bf[0]), planes(minus_d[:, :, halves[0]]), gain, ALU.mult)
        st_step(3)
        nc.vector.tensor_tensor(woven(z_bf[1]), planes(minus_d[:, :, halves[1]]), gain, ALU.mult)

        st_n5 = [
            keep.tile([P, PACK, S // 2], F32, name="st_n5_0"),
            keep.tile([P, PACK, S // 2], F32, name="st_n5_1", tag="gate3"),
        ]
        for a in range(2):
            for t in range(PACK):
                nc.scalar.activation(st_n5[a][:, t, :], st[:, t, :].indirect(n5_t[:, 16 * a : 16 * (a + 1)]), ACT.Copy)

        w_bf_rest = keep.tile([P, 3 * 2 * PACK * P], BF16, name="w_bf_rest", tag="s3", align_bytes=64)
        w_bf = [w_bf_first[:]] + [w_bf_rest[:, 2 * PACK * P * a : 2 * PACK * P * (a + 1)] for a in range(3)]
        for t in range(1, PACK):
            cast_w(t, nc.scalar.copy, w_bf[t])

        def quantize_w(t):
            quantize_part(w_q, slice(2 * P * t, 2 * P * (t + 1)), w_bf[t])

        def z2_step(a):
            nc.vector.tensor_tensor(woven(z2_bf[a]), planes(st[:, :, halves[a]]), planes(st_n5[a][:]), ALU.subtract)

        quantize_part(z_q, halves[0], z_bf[0][:])
        quantize_w(0)
        z2_step(0)
        quantize_part(z_q, halves[1], z_bf[1][:])
        quantize_part(z2_q, halves[0], z2_bf[0][:])
        z2_step(1)
        quantize_w(1)
        quantize_part(z2_q, halves[1], z2_bf[1][:])
        h_bank = [psum.tile([P, S], F32, name="y_bank%d" % t) for t in range(PACK)]

        def h_product(t):
            if t > 1:
                quantize_w(t)
            product(h_bank[t], w_q, 2 * t, z_q, True, False)
            if t == 0:
                product(h_bank[t], w_q, 1, z2_q, False, False, halves[0])
                product(h_bank[t], w_q, 1, z2_q, False, True, halves[1])
            else:
                product(h_bank[t], w_q, 2 * t + 1, z2_q, False, True)

        h = [keep.tile([P, NARROW], F32, name="h%d" % t) for t in range(PACK)]
        members = [keep.tile([P, W], F32, name="members%d" % t) for t in range(PACK)]
        pieces = [halves] * PACK

        def fetch(t, group):
            for cols in group:
                window = h[t][:].indirect(n6_t[:, cols.start // 8 : cols.stop // 8])
                dst = members[t][:, 2 * cols.start : 2 * cols.stop]
                if t == 0:
                    nc.vector.tensor_copy(dst, window)
                else:
                    nc.scalar.activation(dst, window, ACT.Copy)

        def finish(t, group):
            top = [ring.tile([P, c.stop - c.start], F32, name="top") for c in group]
            rest = [ring.tile([P, c.stop - c.start], F32, name="rest") for c in group]
            result = [ring.tile([P, c.stop - c.start], F32, name="result") for c in group]
            first = [members[t][:, 2 * c.start : 2 * c.stop : 2] for c in group]
            second = [members[t][:, 2 * c.start + 1 : 2 * c.stop : 2] for c in group]
            for a, cols in enumerate(group):
                nc.vector.tensor_tensor(top[a][:], h[t][:, cols], first[a], ALU.max)
            for a, cols in enumerate(group):
                nc.vector.tensor_tensor(rest[a][:], second[a], top[a][:], ALU.subtract)
            for a, cols in enumerate(group):
                nc.vector.scalar_tensor_tensor(result[a][:], rest[a][:], 0.0, first[a], ALU.min, ALU.add)
                nc.sync.dma_start(out[P * t : P * (t + 1), cols], result[a][:])

        h_product(0)
        h_product(1)
        h_product(2)
        nc.vector.tensor_copy(h[0][:, :S], h_bank[0][:])
        h_product(3)
        fetch(0, halves)
        nc.scalar.copy(h[1][:, :S], h_bank[1][:])
        for t in range(1, PACK):
            fetch(t, halves[:1])
            if t + 1 < PACK:
                nc.scalar.copy(h[t + 1][:, :S], h_bank[t + 1][:])
            fetch(t, halves[1:])
        for t in range(PACK):
            finish(t, halves)
